import numpy as np
CORES = [7,15,23,31,135,143,151,159,167,175,183,191,199,207,215,223,231,239,247,255]
N = 20
def setup_inputs(rng):
    return {"x": rng.standard_normal((N, 128, 128), dtype=np.float32)}
def reference(x):
    g = np.concatenate(list(x), axis=1)
    return {"y": np.broadcast_to(g, (N,) + g.shape)}

@@ -1,0 +1,22 @@
+SCRATCH = {
+    "img": ("sbuf", [128, 2560], "float32"),
+}
+SEMAPHORES = ["loaded", "sent", "arrived", "stored"]
+
+
+def rank_program(g, core, T, topo):
+    rank = T.rank_of(core)
+    if rank is None:
+        return
+    n = len(T.cores)
+    mine = T.img[:, 128 * rank:128 * rank + 128]
+    g.dma_start(mine, T.x[:]).then_inc(T.sem.loaded, 16)
+    g.wait_ge(T.sem.loaded, 16)
+    for k in range(1, n):
+        d = T.cores[(rank + k) % n]
+        rid, pid = topo.addr(d, core)
+        g.remote_dma(mine, mine, T.sem.arrived, T.sem.sent, pid, rid, 0xFF)
+    g.wait_ge(T.sem.sent, 8 * (n - 1))
+    g.wait_ge(T.sem.arrived, 8 * (n - 1))
+    g.dma_start(T.y[:], T.img[:]).then_inc(T.sem.stored, 16)
+    g.wait_ge(T.sem.stored, 16)

@@ -1,22 +1,69 @@
+from concourse.bass import DstId, RemoteDMATransfer
+
+PAIRS = 10
+BLK = 128
+OFFCHIP = 0x00FF
+ENG = 8
+
+RANK, SW0, SW1, RELAY_A, RELAY_B = 7, 6, 1, 2, 3
+LAND = {1: RANK, 2: RANK, 3: RANK, 4: SW0, 5: RELAY_A, 6: RELAY_A, 7: RELAY_A, 8: RELAY_B, 9: RELAY_B}
+SENDS = {SW0: (1, 2, 3, 4), SW1: (5, 6, 7, 8, 9)}
+
 SCRATCH = {
-    "img": ("sbuf", [128, 2560], "float32"),
+    "img": ("sbuf", [128, 2 * PAIRS * BLK], "float32"),
 }
-SEMAPHORES = ["loaded", "sent", "arrived", "stored"]
+SEMAPHORES = ["loaded", "stored", "sent", "arrived"] + ["in%d" % s for s in range(PAIRS)]
 
 
 def rank_program(g, core, T, topo):
-    rank = T.rank_of(core)
-    if rank is None:
+    role = core % 8
+    chip0 = core - role
+    rank = T.rank_of(chip0 + RANK)
+    if rank is None or role not in (RANK, SW0, SW1, RELAY_A, RELAY_B):
         return
-    n = len(T.cores)
-    mine = T.img[:, 128 * rank:128 * rank + 128]
-    g.dma_start(mine, T.x[:]).then_inc(T.sem.loaded, 16)
-    g.wait_ge(T.sem.loaded, 16)
-    for k in range(1, n):
-        d = T.cores[(rank + k) % n]
-        rid, pid = topo.addr(d, core)
-        g.remote_dma(mine, mine, T.sem.arrived, T.sem.sent, pid, rid, 0xFF)
-    g.wait_ge(T.sem.sent, 8 * (n - 1))
-    g.wait_ge(T.sem.arrived, 8 * (n - 1))
-    g.dma_start(T.y[:], T.img[:]).then_inc(T.sem.stored, 16)
-    g.wait_ge(T.sem.stored, 16)
+    p, q = rank // 2, rank % 2
+    my_rank_core = chip0 + RANK
+    mate_rank_core = T.cores[rank ^ 1]
+
+    def blk(j):
+        return T.img[:, BLK * j:BLK * (j + 1)]
+
+    calls = [0]
+
+    def write(j, dests, sem):
+        ids = []
+        for d in dests:
+            rid, pid = topo.addr(d, core)
+            ids.append(DstId(rid=rid, pnc=pid))
+        g.remote_dma_fused(
+            [RemoteDMATransfer(dst_ids=ids, dma_engine_mask=OFFCHIP, remote_sem=sem,
+                               src=blk(j), dsts=[blk(j) for _ in dests])],
+            local_sem=T.sem.sent)
+        calls[0] += 1
+
+    if role == RANK:
+        g.dma_start(blk(rank), T.x[:]).then_inc(T.sem.loaded, 16)
+        g.wait_ge(T.sem.loaded, 16)
+        write(rank, [chip0 + SW0, chip0 + SW1, mate_rank_core], T.sem.arrived)
+
+    if role in SENDS:
+        g.wait_ge(T.sem.arrived, ENG)
+        dests = [T.cores[2 * ((p + d) % PAIRS) + q] - RANK + LAND[d] for d in SENDS[role]]
+        write(rank, dests, T.sem["in%d" % p])
+
+    for d in range(1, PAIRS):
+        if LAND[d] != role:
+            continue
+        s = (p - d) % PAIRS
+        g.wait_ge(T.sem["in%d" % s], ENG)
+        if role == RANK:
+            write(2 * s + q, [mate_rank_core], T.sem.arrived)
+        else:
+            write(2 * s + q, [my_rank_core, mate_rank_core], T.sem.arrived)
+
+    if role == RANK:
+        g.wait_ge(T.sem.arrived, ENG * 16)
+    g.wait_ge(T.sem.sent, ENG * calls[0])
+    if role == RANK:
+        g.dma_start(T.y[:], T.img[:]).then_inc(T.sem.stored, 16)
+        g.wait_ge(T.sem.stored, 16)

@@ -42,7 +42,7 @@ def rank_program(g, core, T, topo):
         calls[0] += 1
 
     if role == RANK:
-        g.dma_start(blk(rank), T.x[:]).then_inc(T.sem.loaded, 16)
+        g.sync.dma_start(blk(rank), T.x[:]).then_inc(T.sem.loaded, 16)
         g.wait_ge(T.sem.loaded, 16)
         write(rank, [chip0 + SW0, chip0 + SW1, mate_rank_core], T.sem.arrived)
 
@@ -60,10 +60,13 @@ def rank_program(g, core, T, topo):
             write(2 * s + q, [mate_rank_core], T.sem.arrived)
         else:
             write(2 * s + q, [my_rank_core, mate_rank_core], T.sem.arrived)
+    g.wait_ge(T.sem.sent, ENG * calls[0])
 
     if role == RANK:
-        g.wait_ge(T.sem.arrived, ENG * 16)
-    g.wait_ge(T.sem.sent, ENG * calls[0])
-    if role == RANK:
-        g.dma_start(T.y[:], T.img[:]).then_inc(T.sem.stored, 16)
-        g.wait_ge(T.sem.stored, 16)
+        g.sync.wait_ge(T.sem.loaded, 16)
+        for d in range(1, PAIRS):
+            if LAND[d] == RANK:
+                g.sync.wait_ge(T.sem["in%d" % ((p - d) % PAIRS)], ENG)
+        g.sync.wait_ge(T.sem.arrived, ENG * 16)
+        g.sync.dma_start(T.y[:], T.img[:]).then_inc(T.sem.stored, 16)
+        g.sync.wait_ge(T.sem.stored, 16)

from concourse.bass import DstId, RemoteDMATransfer

PAIRS = 10
BLK = 128
OFFCHIP = 0x00FF
ENG = 8

RANK, SW0, SW1, RELAY_A, RELAY_B = 7, 6, 1, 2, 3
LAND = {1: RANK, 2: RANK, 3: RANK, 4: SW0, 5: RELAY_A, 6: RELAY_A, 7: RELAY_A, 8: RELAY_B, 9: RELAY_B}
SENDS = {SW0: (1, 2, 3, 4), SW1: (5, 6, 7, 8, 9)}

SCRATCH = {
    "img": ("sbuf", [128, 2 * PAIRS * BLK], "float32"),
}
SEMAPHORES = ["loaded", "stored", "sent", "arrived"] + ["in%d" % s for s in range(PAIRS)]


def rank_program(g, core, T, topo):
    role = core % 8
    chip0 = core - role
    rank = T.rank_of(chip0 + RANK)
    if rank is None or role not in (RANK, SW0, SW1, RELAY_A, RELAY_B):
        return
    p, q = rank // 2, rank % 2
    my_rank_core = chip0 + RANK
    mate_rank_core = T.cores[rank ^ 1]

    def blk(j):
        return T.img[:, BLK * j:BLK * (j + 1)]

    calls = [0]

    def write(j, dests, sem):
        ids = []
        for d in dests:
            rid, pid = topo.addr(d, core)
            ids.append(DstId(rid=rid, pnc=pid))
        g.remote_dma_fused(
            [RemoteDMATransfer(dst_ids=ids, dma_engine_mask=OFFCHIP, remote_sem=sem,
                               src=blk(j), dsts=[blk(j) for _ in dests])],
            local_sem=T.sem.sent)
        calls[0] += 1

    if role == RANK:
        g.sync.dma_start(blk(rank), T.x[:]).then_inc(T.sem.loaded, 16)
        g.wait_ge(T.sem.loaded, 16)
        write(rank, [chip0 + SW0, chip0 + SW1, mate_rank_core], T.sem.arrived)

    if role in SENDS:
        g.wait_ge(T.sem.arrived, ENG)
        dests = [T.cores[2 * ((p + d) % PAIRS) + q] - RANK + LAND[d] for d in SENDS[role]]
        write(rank, dests, T.sem["in%d" % p])

    for d in range(1, PAIRS):
        if LAND[d] != role:
            continue
        s = (p - d) % PAIRS
        g.wait_ge(T.sem["in%d" % s], ENG)
        if role == RANK:
            write(2 * s + q, [mate_rank_core], T.sem.arrived)
        else:
            write(2 * s + q, [my_rank_core, mate_rank_core], T.sem.arrived)
    g.wait_ge(T.sem.sent, ENG * calls[0])

    if role == RANK:
        g.sync.wait_ge(T.sem.loaded, 16)
        for d in range(1, PAIRS):
            if LAND[d] == RANK:
                g.sync.wait_ge(T.sem["in%d" % ((p - d) % PAIRS)], ENG)
        g.sync.wait_ge(T.sem.arrived, ENG * 16)
        g.sync.dma_start(T.y[:], T.img[:]).then_inc(T.sem.stored, 16)
        g.sync.wait_ge(T.sem.stored, 16)
